import numpy as np, ml_dtypes
CORES = [35,38,43,46]
N = 4
import mx_ref
BF = ml_dtypes.bfloat16
def cols(t, e):
    v = np.concatenate([t.reshape(128, -1, 4), np.zeros((128, 1, 4), BF)], axis=1)
    return np.ascontiguousarray(v[:, e]).reshape(128, -1)
def f(rng, *shape):
    return mx_ref.flush((rng.standard_normal(shape, dtype=np.float32) * np.exp2(rng.integers(-2, 3, shape[:-1] + (1,)))).astype(BF))
def wide(rng, *shape, cols=0):
    v = rng.standard_normal(shape, dtype=np.float32) * np.exp2(rng.integers(-12, 13, shape)).astype(np.float32)
    if cols: v *= np.repeat(np.exp2(rng.integers(-cols, cols + 1, shape[:-2] + (1, shape[-1] // 4))) * (rng.random(shape[:-2] + (1, shape[-1] // 4)) > 0.0625), 4, axis=-1).astype(np.float32)
    return mx_ref.flush(v.astype(BF))
T, NBIT, K, O = 384, 9, 512, 2
def planes(rng):
    v = np.zeros((N, 128, 512), BF); v[:, :, :4 * NBIT] = f(rng, N, 128, 4 * NBIT); return v
def setup_inputs(rng):
    return {"x": f(rng, N, 128, 4 * T), "hp": planes(rng), "e": f(rng, N, 128, 4 * K), "qw": f(rng, N, 128, O * 512)}
def setup_inputs_zero(rng):
    d = setup_inputs(rng)
    for r in rng.permutation(N)[:N // 2]:
        i = rng.integers(0, NBIT); d["hp"][r, :, 4 * i:4 * i + 4] = 0
    for r in range(N):
        for j in rng.permutation(T)[:T // 8]: d["x"][r, :, 4 * j:4 * j + 4] = 0
    return d
def setup_inputs_onebucket(rng):
    d = setup_inputs(rng); d["x"] = np.tile(d["hp"][rng.integers(0, N)][:, :4], (N, 1, T)); return d
def setup_inputs_all(rng):
    d = setup_inputs(rng); g = f(rng, 128, 4).astype(np.float32)[None, :, None, :]
    d["hp"][:, :, :4 * NBIT] = (g * np.exp2(rng.integers(0, 4, (N, 1, NBIT, 1)))).reshape(N, 128, -1).astype(BF)
    s = np.stack([rng.permutation(T) % 2 * 2 - 1 for r in range(N)]) * np.exp2(rng.integers(0, 4, (N, T)))
    d["x"] = (g * s[:, None, :, None]).reshape(N, 128, -1).astype(BF); return d
def setup_inputs_small(rng):
    d = setup_inputs(rng)
    for k in ("x", "hp"):
        v = d[k].astype(np.float32) * np.float32(2.0 ** -24)
        d[k] = mx_ref.flush(np.where(np.abs(v) < np.float32(2.0 ** -30), np.float32(0), v).astype(BF))
    return d
def setup_inputs_spread(rng):
    d = setup_inputs(rng); d["x"] = wide(rng, N, 128, 4 * T, cols=8); d["e"] = wide(rng, N, 128, 4 * K, cols=8); return d
def check_inputs(d):
    b = []
    if (np.asarray(d["hp"]).astype(np.float32)[:, :, 4 * NBIT:] != 0).any(): b.append("hp")
    return b
def reference(x, hp, e, qw):
    X = [mx_ref.quantize(x[r]) for r in range(N)]
    H = [mx_ref.quantize(hp[q]) for q in range(N)]
    W = [[mx_ref.quantize(np.ascontiguousarray(qw[r][:, 512 * o:512 * o + 512])) for o in range(O)] for r in range(N)]
    y = np.zeros((N, 128, N * O * T), np.float32); bk = np.zeros((N, N, T), np.float32)
    for r in range(N):
        for q in range(N):
            s = mx_ref.matmul(H[q], X[r])
            b = np.zeros(T, int)
            for i in range(NBIT): b += 2 ** i * (s[i] > 0)
            bk[r, q] = b
            c = mx_ref.quantize(cols(e[q], b))
            for o in range(O):
                k = (q * O + o) * T
                y[r][:, k:k + T] = mx_ref.matmul(W[r][o], c)
    return {"y": y, "bk": bk}

@@ -1,0 +1,273 @@
+from concourse.bass import DstId, RemoteDMATransfer
+from concourse.mybir import dt, AluOpType, ActivationFunctionType
+
+TOK, NBIT, KCOL, OUT = 384, 9, 512, 2
+SLOT = 10
+BLK = 32
+PRE = 96
+LAND = PRE + 128
+ZFROM = LAND + 3 * SLOT
+HCOLS = LAND + 128
+HALF = KCOL // 2
+RUNS = TOK // 16
+FREE = RUNS * BLK
+
+_X4 = "float8_e4m3fn_x4"
+SCRATCH = {
+    "hb": ("sbuf", [128, 4 * LAND], "bfloat16"),
+    "xb": ("sbuf", [128, 4 * TOK], "bfloat16"),
+    "wb": ("sbuf", [128, 4 * 128 * OUT], "bfloat16"),
+    "eb": ("sbuf", [128, 4 * KCOL], "bfloat16"),
+    "HC": ("sbuf", [128, HCOLS], _X4), "HS": ("sbuf", [128, HCOLS], "uint8"),
+    "XC": ("sbuf", [128, TOK], _X4), "XS": ("sbuf", [128, TOK], "uint8"),
+    "WC": ("sbuf", [128, 128 * OUT], _X4), "WS": ("sbuf", [128, 128 * OUT], "uint8"),
+    "mul": ("sbuf", [128, FREE], "bfloat16"),
+    "bf": ("sbuf", [128, 4, BLK], "float32"), "tb": ("sbuf", [128, 4, BLK], "float32"),
+    "offo": ("sbuf", [128, RUNS], "uint16"), "offr": ("sbuf", [128, 3 * RUNS], "uint16"),
+    "yst": ("sbuf", [128, 4 * OUT * TOK], "float32"),
+}
+for _k in range(4):
+    SCRATCH["EC%d" % _k] = ("sbuf", [128, KCOL], _X4)
+    SCRATCH["ES%d" % _k] = ("sbuf", [128, KCOL], "uint8")
+    for _o in range(OUT):
+        SCRATCH["G%d%d" % (_k, _o)] = ("sbuf", [128, KCOL], "float32")
+for _k in range(2):
+    SCRATCH["bits%d" % _k] = ("sbuf", [128, RUNS, BLK], "bfloat16")
+    SCRATCH["tr%d" % _k] = ("sbuf", [128, FREE], "bfloat16")
+    SCRATCH["sc%d" % _k] = ("sbuf", [128, FREE], "float32")
+for _k in range(8):
+    SCRATCH["p%d" % _k] = ("psum", [128, 512], "float32")
+
+SEMAPHORES = (["l_hp", "l_e0", "l_e1", "l_x", "l_w", "zc", "st", "st2", "sent", "hpin", "nbin", "m0", "m1", "d0", "d1",
+               "q_hp", "q_e0", "q_e1", "q_x", "q_w", "k_a", "k_mul", "k_bf", "t_o", "t_r", "bfc", "v_tb",
+               "bit0", "bit1", "trn0", "trn1", "scn0", "scn1", "off0", "off1"]
+              + ["t%d%d" % (k, o) for k in range(4) for o in range(OUT)]
+              + ["c%d%d" % (k, o) for k in range(4) for o in range(OUT)]
+              + ["y%d%d" % (k, o) for k in range(4) for o in range(OUT)])
+
+
+def _bits(engines):
+    return sum(1 << e for e in engines)
+
+
+def rank_program(g, core, T, topo):
+    rank = T.rank_of(core)
+    if rank is None:
+        return
+    S = T.sem
+    nb = mate = diag = None
+    for c in T.cores:
+        if c == core:
+            continue
+        if topo.chip(c) == topo.chip(core):
+            nb = c
+        elif topo.die(c) == topo.die(core):
+            mate = c
+        else:
+            diag = c
+    off = topo.engines(core, mate)
+    on = [e for e in topo.engines(core, nb) if e not in off]
+    oh = len(off) // 2
+    ranks = [rank, T.rank_of(nb), T.rank_of(mate), T.rank_of(diag)]
+    u8 = dt.uint8
+    sent = [0]
+
+    def cd(name, a, b):
+        return T[name][:, a:b].bitcast(u8)
+
+    def pl(name, a, b):
+        return T[name][:, a:b]
+
+    def send(*moves):
+        tr = []
+        for dst, eng, sem, src, out in moves:
+            a = topo.addr(dst)
+            tr.append(RemoteDMATransfer(dst_ids=[DstId(rid=a[0], pnc=a[1])], dma_engine_mask=_bits(eng),
+                                        remote_sem=S[sem], srcs=[src], dsts=[out]))
+            sent[0] += len(eng)
+        g.remote_dma_fused(tr, local_sem=S.sent)
+
+    y = g.sync
+    y.dma_start(T.eb[:, 0:4 * HALF], T.e[:, 0:4 * HALF]).then_inc(S.l_e0, 16)
+    y.dma_start(T.eb[:, 4 * HALF:], T.e[:, 4 * HALF:]).then_inc(S.l_e1, 16)
+    y.dma_start(T.wb[:, :], T.qw[:, :]).then_inc(S.l_w, 16)
+    a = g.scalar
+    a.dma_start(T.hb[:, 4 * PRE:], T.hp[:, :]).then_inc(S.l_hp, 16)
+    a.dma_start(T.hb[:, 0:4 * PRE], T.hp[:, 512 - 4 * PRE:512]).then_inc(S.l_hp, 16)
+    a.dma_start(T.xb[:, :], T.x[:, :]).then_inc(S.l_x, 16)
+    nz = HCOLS - ZFROM
+    z0 = PRE + SLOT
+    y.wait_ge(S.q_hp, 1)
+    y.dma_start(cd("HC", ZFROM, HCOLS), cd("HC", z0, z0 + nz)).then_inc(S.zc, 16)
+    y.dma_start(pl("HS", ZFROM, HCOLS), pl("HS", z0, z0 + nz)).then_inc(S.zc, 16)
+
+    slots = [(nb, on, 0), (mate, off[:oh], 1), (diag, off[oh:], 2)]
+    g.wait_ge(S.q_hp, 1)
+    for view, name in ((cd, "HC"), (pl, "HS")):
+        send(*[(d, en, "hpin", view(name, PRE, PRE + SLOT), view(name, LAND + SLOT * k, LAND + SLOT * (k + 1)))
+               for d, en, k in slots])
+    g.wait_ge(S.q_e0, 1)
+    send((mate, off, "m0", cd("EC0", 0, HALF), cd("EC2", 0, HALF)), (nb, on, "nbin", cd("EC0", 0, HALF), cd("EC1", 0, HALF)))
+    g.wait_ge(S.q_e1, 1)
+    send((mate, off, "m1", cd("EC0", HALF, KCOL), cd("EC2", HALF, KCOL)),
+         (nb, on, "nbin", cd("EC0", HALF, KCOL), cd("EC1", HALF, KCOL)))
+    send((mate, off, "m1", pl("ES0", 0, KCOL), pl("ES2", 0, KCOL)), (nb, on, "nbin", pl("ES0", 0, KCOL), pl("ES1", 0, KCOL)))
+    send((diag, off, "d1", cd("EC0", HALF, KCOL), cd("EC3", HALF, KCOL)))
+    send((diag, off, "d1", pl("ES0", 0, KCOL), pl("ES3", 0, KCOL)))
+    g.wait_ge(S.m0, len(off))
+    send((nb, on, "d0", cd("EC2", 0, HALF), cd("EC3", 0, HALF)))
+    g.wait_ge(S.sent, sent[0])
+
+    t = g.tensor
+
+    def planes(bank, first, sem):
+        for b in range(4):
+            f = first - BLK * b
+            m = t.matmul_mx(T[bank][:, 0:TOK], T.HC[:, f:f + 128], T.HS[:, f:f + 128], T.XC[:, 0:TOK], T.XS[:, 0:TOK],
+                            b == 0, b == 3)
+        m.then_inc(S[sem], 1)
+
+    def tables(k, banks):
+        for o in range(OUT):
+            w = slice(128 * o, 128 * o + 128)
+            t.matmul_mx(T[banks[o]][:, 0:KCOL], T.WC[:, w], T.WS[:, w], T["EC%d" % k][:, 0:KCOL], T["ES%d" % k][:, 0:KCOL],
+                        True, True).then_inc(S["t%d%d" % (k, o)], 1)
+
+    t.wait_ge(S.q_hp, 1)
+    t.wait_ge(S.q_x, 1)
+    planes("p0", PRE, "t_o")
+    t.wait_ge(S.q_e0, 1)
+    t.wait_ge(S.q_e1, 1)
+    t.wait_ge(S.q_w, 1)
+    tables(0, ("p2", "p3"))
+    t.wait_ge(S.zc, 32)
+    t.wait_ge(S.hpin, 2 * (len(on) + 2 * oh))
+    planes("p1", LAND, "t_r")
+    t.wait_ge(S.nbin, 3 * len(on))
+    tables(1, ("p4", "p5"))
+    t.wait_ge(S.m0, len(off))
+    t.wait_ge(S.m1, 2 * len(off))
+    tables(2, ("p6", "p7"))
+    t.wait_ge(S.c00, 1)
+    t.wait_ge(S.c01, 1)
+    t.wait_ge(S.d1, 2 * len(off))
+    t.wait_ge(S.d0, len(on))
+    tables(3, ("p2", "p3"))
+    bank = {(0, 0): "p2", (0, 1): "p3", (1, 0): "p4", (1, 1): "p5", (2, 0): "p6", (2, 1): "p7", (3, 0): "p2", (3, 1): "p3"}
+
+    def col(k, o):
+        c = (ranks[k] * OUT + o) * TOK
+        return slice(c, c + TOK)
+
+    def lst(k):
+        return T.offo[:, 0:RUNS] if k == 0 else T.offr[:, RUNS * (k - 1):RUNS * k]
+
+    def pick(k, o):
+        return T["G%d%d" % (k, o)][:, 0:KCOL].indirect(lst(k))
+
+    def lists_made(q, k):
+        if k == 0:
+            q.wait_ge(S.off0, 1)
+        else:
+            q.wait_ge(S.off1, 3)
+
+    v = g.vector
+    gt, mu, ad = AluOpType.is_gt, AluOpType.mult, AluOpType.add
+
+    def vcopy(k, o):
+        v.wait_ge(S["t%d%d" % (k, o)], 1)
+        v.tensor_copy(T["G%d%d" % (k, o)][:, 0:KCOL], T[bank[k, o]][:, 0:KCOL]).then_inc(S["c%d%d" % (k, o)], 1)
+
+    def vpick(k, o):
+        lists_made(v, k)
+        v.wait_ge(S["c%d%d" % (k, o)], 1)
+        v.tensor_copy(T.yst[:, col(k, o)], pick(k, o)).then_inc(S["y%d%d" % (k, o)], 1)
+
+    def buckets(n, p, sem):
+        bt, tr, sc = T["bits%d" % n], T["tr%d" % n], T["sc%d" % n]
+        v.wait_ge(S[sem], 1)
+        for h in range(2):
+            v.tensor_scalar(bt[:, :, 16 * h:16 * h + 16], T[p][:, 0:TOK], 0.0, None, gt).then_inc(S["bit%d" % n], 1)
+        v.wait_ge(S["bit%d" % n], 2)
+        v.transpose(tr[:, :], bt[:, :, :]).then_inc(S["trn%d" % n], 1)
+        v.wait_ge(S["trn%d" % n], 1)
+        v.tensor_tensor_scan(sc[:, :], T.mul[:, :], tr[:, :], 0.0, mu, ad).then_inc(S["scn%d" % n], 1)
+        v.wait_ge(S["scn%d" % n], 1)
+
+    v.memset(T.mul[:, :], 0.5).then_inc(S.k_a, 1)
+    v.wait_ge(S.k_a, 1)
+    for k in range(3):
+        v.memset(T.mul[:, SLOT * k:FREE:BLK], 0.0).then_inc(S.k_mul, 1)
+    v.memset(T.bf[:, :, :], 0.0).then_inc(S.k_bf, 1)
+    v.wait_ge(S.l_hp, 32)
+    v.quantize_mx(T.HC[:, 0:LAND], T.HS[:, 0:LAND], T.hb[:, :]).then_inc(S.q_hp, 1)
+    for h in range(2):
+        c = slice(HALF * h, HALF * h + HALF)
+        v.wait_ge(S["l_e%d" % h], 16)
+        v.quantize_mx(T.EC0[:, c], T.ES0[:, c], T.eb[:, 4 * HALF * h:4 * HALF * (h + 1)]).then_inc(S["q_e%d" % h], 1)
+    v.wait_ge(S.l_x, 16)
+    v.quantize_mx(T.XC[:, :], T.XS[:, :], T.xb[:, :]).then_inc(S.q_x, 1)
+    v.wait_ge(S.l_w, 16)
+    v.quantize_mx(T.WC[:, :], T.WS[:, :], T.wb[:, :]).then_inc(S.q_w, 1)
+    v.wait_ge(S.k_mul, 3)
+    buckets(0, "p0", "t_o")
+    v.tensor_scalar(T.offo[:, 0:RUNS], T.sc0[:, NBIT - 1:FREE:BLK], 256.0, None, mu).then_inc(S.off0, 1)
+    buckets(1, "p1", "t_r")
+    for k in range(3):
+        v.tensor_scalar(T.offr[:, RUNS * k:RUNS * (k + 1)], T.sc1[:, SLOT * k + NBIT - 1:FREE:BLK], 256.0, None,
+                        mu).then_inc(S.off1, 1)
+    vpick(1, 0)
+    v.wait_ge(S.k_bf, 1)
+    v.wait_ge(S.off0, 1)
+    v.tensor_copy(T.bf[0:BLK, 0, 0:RUNS], T.offo[0:BLK, :]).then_inc(S.bfc, 1)
+    for k in range(1, 4):
+        v.tensor_copy(T.bf[0:BLK, k, 0:RUNS], T.offr[0:BLK, RUNS * (k - 1):RUNS * k]).then_inc(S.bfc, 1)
+    v.wait_ge(S.bfc, 4)
+    v.transpose(T.tb[0:BLK, :, :], T.bf[0:BLK, :, :]).then_inc(S.v_tb, 1)
+    vpick(2, 0)
+    vcopy(3, 0)
+    vpick(3, 0)
+
+    cp = ActivationFunctionType.Copy
+
+    def acopy(k, o):
+        a.wait_ge(S["t%d%d" % (k, o)], 1)
+        a.activation(T["G%d%d" % (k, o)][:, 0:KCOL], T[bank[k, o]][:, 0:KCOL], cp).then_inc(S["c%d%d" % (k, o)], 1)
+
+    def apick(k, o):
+        lists_made(a, k)
+        a.wait_ge(S["c%d%d" % (k, o)], 1)
+        a.activation(T.yst[:, col(k, o)], pick(k, o), cp).then_inc(S["y%d%d" % (k, o)], 1)
+
+    acopy(0, 0)
+    acopy(0, 1)
+    apick(0, 0)
+    apick(0, 1)
+    acopy(1, 0)
+    acopy(1, 1)
+    apick(1, 1)
+    acopy(2, 0)
+    acopy(2, 1)
+    apick(2, 1)
+    acopy(3, 1)
+    apick(3, 1)
+    a.wait_ge(S.y31, 1)
+    a.dma_start(T.y[:, col(3, 1)], T.yst[:, col(3, 1)]).then_inc(S.st2, 16)
+    a.wait_ge(S.st2, 16)
+
+    n = [0]
+
+    def store(k, o):
+        y.wait_ge(S["y%d%d" % (k, o)], 1)
+        y.dma_start(T.y[:, col(k, o)], T.yst[:, col(k, o)]).then_inc(S.st, 16)
+        n[0] += 16
+
+    for k, o in ((0, 0), (0, 1), (1, 0), (1, 1)):
+        store(k, o)
+    y.wait_ge(S.v_tb, 1)
+    for k in range(4):
+        y.dma_start(T.bk[ranks[k]:ranks[k] + 1, :], T.tb[0:RUNS, k, 0:16]).then_inc(S.st, 16)
+        n[0] += 16
+    for k, o in ((2, 0), (2, 1), (3, 0)):
+        store(k, o)
+    y.wait_ge(S.st, n[0])

@@ -4,17 +4,21 @@ from concourse.mybir import dt, AluOpType, ActivationFunctionType
 TOK, NBIT, KCOL, OUT = 384, 9, 512, 2
 SLOT = 10
 BLK = 32
-PRE = 96
-LAND = PRE + 128
+HPC = 16
+LAND = 128
 ZFROM = LAND + 3 * SLOT
-HCOLS = LAND + 128
+OWN = LAND + 128
+HCOLS = OWN + 128
 HALF = KCOL // 2
 RUNS = TOK // 16
 FREE = RUNS * BLK
+SUB = TOK // 3
+PART = TOK // 2
 
 _X4 = "float8_e4m3fn_x4"
 SCRATCH = {
-    "hb": ("sbuf", [128, 4 * LAND], "bfloat16"),
+    "hb": ("sbuf", [128, 512], "bfloat16"), "h4": ("sbuf", [128, 4 * LAND + 512], "bfloat16"),
+    "HQ": ("sbuf", [128, 128], _X4), "HQS": ("sbuf", [128, 128], "uint8"),
     "xb": ("sbuf", [128, 4 * TOK], "bfloat16"),
     "wb": ("sbuf", [128, 4 * 128 * OUT], "bfloat16"),
     "eb": ("sbuf", [128, 4 * KCOL], "bfloat16"),
@@ -22,6 +26,10 @@ SCRATCH = {
     "XC": ("sbuf", [128, TOK], _X4), "XS": ("sbuf", [128, TOK], "uint8"),
     "WC": ("sbuf", [128, 128 * OUT], _X4), "WS": ("sbuf", [128, 128 * OUT], "uint8"),
     "mul": ("sbuf", [128, FREE], "bfloat16"),
+    "bits0": ("sbuf", [128, SUB // 16, BLK], "bfloat16"), "tr0": ("sbuf", [128, 2 * SUB], "bfloat16"),
+    "sc0": ("sbuf", [128, 2 * SUB], "float32"),
+    "bits1": ("sbuf", [128, RUNS, BLK], "bfloat16"), "tr1": ("sbuf", [128, FREE], "bfloat16"),
+    "sc1": ("sbuf", [128, FREE], "float32"),
     "bf": ("sbuf", [128, 4, BLK], "float32"), "tb": ("sbuf", [128, 4, BLK], "float32"),
     "offo": ("sbuf", [128, RUNS], "uint16"), "offr": ("sbuf", [128, 3 * RUNS], "uint16"),
     "yst": ("sbuf", [128, 4 * OUT * TOK], "float32"),
@@ -31,16 +39,13 @@ for _k in range(4):
     SCRATCH["ES%d" % _k] = ("sbuf", [128, KCOL], "uint8")
     for _o in range(OUT):
         SCRATCH["G%d%d" % (_k, _o)] = ("sbuf", [128, KCOL], "float32")
-for _k in range(2):
-    SCRATCH["bits%d" % _k] = ("sbuf", [128, RUNS, BLK], "bfloat16")
-    SCRATCH["tr%d" % _k] = ("sbuf", [128, FREE], "bfloat16")
-    SCRATCH["sc%d" % _k] = ("sbuf", [128, FREE], "float32")
 for _k in range(8):
     SCRATCH["p%d" % _k] = ("psum", [128, 512], "float32")
 
 SEMAPHORES = (["l_hp", "l_e0", "l_e1", "l_x", "l_w", "zc", "st", "st2", "sent", "hpin", "nbin", "m0", "m1", "d0", "d1",
-               "q_hp", "q_e0", "q_e1", "q_x", "q_w", "k_a", "k_mul", "k_bf", "t_o", "t_r", "bfc", "v_tb",
-               "bit0", "bit1", "trn0", "trn1", "scn0", "scn1", "off0", "off1"]
+               "q_z", "q_hp", "q_h4", "q_e0", "q_e1", "q_x", "q_w", "k_z", "k_h", "h4c", "k_a", "k_mul", "k_bf",
+               "t_o", "t_r0", "t_r1", "bfc", "v_tb",
+               "bit0", "bit1", "bit2", "trn0", "trn1", "scn0", "scn1", "off0", "off1", "off2", "off3"]
               + ["t%d%d" % (k, o) for k in range(4) for o in range(OUT)]
               + ["c%d%d" % (k, o) for k in range(4) for o in range(OUT)]
               + ["y%d%d" % (k, o) for k in range(4) for o in range(OUT)])
@@ -55,6 +60,7 @@ def rank_program(g, core, T, topo):
     if rank is None:
         return
     S = T.sem
+    cp = ActivationFunctionType.Copy
     nb = mate = diag = None
     for c in T.cores:
         if c == core:
@@ -92,19 +98,17 @@ def rank_program(g, core, T, topo):
     y.dma_start(T.eb[:, 4 * HALF:], T.e[:, 4 * HALF:]).then_inc(S.l_e1, 16)
     y.dma_start(T.wb[:, :], T.qw[:, :]).then_inc(S.l_w, 16)
     a = g.scalar
-    a.dma_start(T.hb[:, 4 * PRE:], T.hp[:, :]).then_inc(S.l_hp, 16)
-    a.dma_start(T.hb[:, 0:4 * PRE], T.hp[:, 512 - 4 * PRE:512]).then_inc(S.l_hp, 16)
+    a.dma_start(T.hb[:, 0:4 * HPC], T.hp[:, 0:4 * HPC]).then_inc(S.l_hp, 16)
     a.dma_start(T.xb[:, :], T.x[:, :]).then_inc(S.l_x, 16)
-    nz = HCOLS - ZFROM
-    z0 = PRE + SLOT
-    y.wait_ge(S.q_hp, 1)
-    y.dma_start(cd("HC", ZFROM, HCOLS), cd("HC", z0, z0 + nz)).then_inc(S.zc, 16)
-    y.dma_start(pl("HS", ZFROM, HCOLS), pl("HS", z0, z0 + nz)).then_inc(S.zc, 16)
+    nz = OWN - ZFROM
+    y.wait_ge(S.q_z, 1)
+    y.dma_start(cd("HC", ZFROM, OWN), cd("HC", 0, nz)).then_inc(S.zc, 16)
+    y.dma_start(pl("HS", ZFROM, OWN), pl("HS", 0, nz)).then_inc(S.zc, 16)
 
     slots = [(nb, on, 0), (mate, off[:oh], 1), (diag, off[oh:], 2)]
     g.wait_ge(S.q_hp, 1)
-    for view, name in ((cd, "HC"), (pl, "HS")):
-        send(*[(d, en, "hpin", view(name, PRE, PRE + SLOT), view(name, LAND + SLOT * k, LAND + SLOT * (k + 1)))
+    for view, src, name in ((cd, "HQ", "HC"), (pl, "HQS", "HS")):
+        send(*[(d, en, "hpin", view(src, 0, SLOT), view(name, LAND + SLOT * k, LAND + SLOT * (k + 1)))
                for d, en, k in slots])
     g.wait_ge(S.q_e0, 1)
     send((mate, off, "m0", cd("EC0", 0, HALF), cd("EC2", 0, HALF)), (nb, on, "nbin", cd("EC0", 0, HALF), cd("EC1", 0, HALF)))
@@ -120,11 +124,10 @@ def rank_program(g, core, T, topo):
 
     t = g.tensor
 
-    def planes(bank, first, sem):
-        for b in range(4):
-            f = first - BLK * b
-            m = t.matmul_mx(T[bank][:, 0:TOK], T.HC[:, f:f + 128], T.HS[:, f:f + 128], T.XC[:, 0:TOK], T.XS[:, 0:TOK],
-                            b == 0, b == 3)
+    def planes(bank, moves, sem):
+        for i, (f, x0, n) in enumerate(moves):
+            m = t.matmul_mx(T[bank][:, 0:n], T.HC[:, f:f + 128], T.HS[:, f:f + 128], T.XC[:, x0:x0 + n], T.XS[:, x0:x0 + n],
+                            i == 0, i == len(moves) - 1)
         m.then_inc(S[sem], 1)
 
     def tables(k, banks):
@@ -133,27 +136,30 @@ def rank_program(g, core, T, topo):
             t.matmul_mx(T[banks[o]][:, 0:KCOL], T.WC[:, w], T.WS[:, w], T["EC%d" % k][:, 0:KCOL], T["ES%d" % k][:, 0:KCOL],
                         True, True).then_inc(S["t%d%d" % (k, o)], 1)
 
-    t.wait_ge(S.q_hp, 1)
+    t.wait_ge(S.q_h4, 1)
     t.wait_ge(S.q_x, 1)
-    planes("p0", PRE, "t_o")
+    t.wait_ge(S.q_z, 1)
+    t.wait_ge(S.zc, 32)
+    planes("p0", [(OWN - SLOT * s, SUB * s, SUB) for s in range(3)], "t_o")
     t.wait_ge(S.q_e0, 1)
     t.wait_ge(S.q_e1, 1)
     t.wait_ge(S.q_w, 1)
     tables(0, ("p2", "p3"))
-    t.wait_ge(S.zc, 32)
     t.wait_ge(S.hpin, 2 * (len(on) + 2 * oh))
-    planes("p1", LAND, "t_r")
+    for h in range(2):
+        planes(("p1", "p4")[h], [(LAND - BLK * b, PART * h, PART) for b in range(4)], "t_r%d" % h)
     t.wait_ge(S.nbin, 3 * len(on))
-    tables(1, ("p4", "p5"))
+    tables(1, ("p5", "p6"))
     t.wait_ge(S.m0, len(off))
     t.wait_ge(S.m1, 2 * len(off))
-    tables(2, ("p6", "p7"))
+    t.wait_ge(S.bit0, 2)
+    tables(2, ("p7", "p0"))
     t.wait_ge(S.c00, 1)
     t.wait_ge(S.c01, 1)
     t.wait_ge(S.d1, 2 * len(off))
     t.wait_ge(S.d0, len(on))
     tables(3, ("p2", "p3"))
-    bank = {(0, 0): "p2", (0, 1): "p3", (1, 0): "p4", (1, 1): "p5", (2, 0): "p6", (2, 1): "p7", (3, 0): "p2", (3, 1): "p3"}
+    bank = {(0, 0): "p2", (0, 1): "p3", (1, 0): "p5", (1, 1): "p6", (2, 0): "p7", (2, 1): "p0", (3, 0): "p2", (3, 1): "p3"}
 
     def col(k, o):
         c = (ranks[k] * OUT + o) * TOK
@@ -165,11 +171,8 @@ def rank_program(g, core, T, topo):
     def pick(k, o):
         return T["G%d%d" % (k, o)][:, 0:KCOL].indirect(lst(k))
 
-    def lists_made(q, k):
-        if k == 0:
-            q.wait_ge(S.off0, 1)
-        else:
-            q.wait_ge(S.off1, 3)
+    def list_made(q, k):
+        q.wait_ge(S["off%d" % k], 3 if k == 0 else 1)
 
     v = g.vector
     gt, mu, ad = AluOpType.is_gt, AluOpType.mult, AluOpType.add
@@ -179,75 +182,93 @@ def rank_program(g, core, T, topo):
         v.tensor_copy(T["G%d%d" % (k, o)][:, 0:KCOL], T[bank[k, o]][:, 0:KCOL]).then_inc(S["c%d%d" % (k, o)], 1)
 
     def vpick(k, o):
-        lists_made(v, k)
+        list_made(v, k)
         v.wait_ge(S["c%d%d" % (k, o)], 1)
         v.tensor_copy(T.yst[:, col(k, o)], pick(k, o)).then_inc(S["y%d%d" % (k, o)], 1)
 
-    def buckets(n, p, sem):
-        bt, tr, sc = T["bits%d" % n], T["tr%d" % n], T["sc%d" % n]
+    def turn(p, n, sem, bt, r0, sb, tr, st):
+        r1 = r0 + n // 16
         v.wait_ge(S[sem], 1)
         for h in range(2):
-            v.tensor_scalar(bt[:, :, 16 * h:16 * h + 16], T[p][:, 0:TOK], 0.0, None, gt).then_inc(S["bit%d" % n], 1)
-        v.wait_ge(S["bit%d" % n], 2)
-        v.transpose(tr[:, :], bt[:, :, :]).then_inc(S["trn%d" % n], 1)
-        v.wait_ge(S["trn%d" % n], 1)
-        v.tensor_tensor_scan(sc[:, :], T.mul[:, :], tr[:, :], 0.0, mu, ad).then_inc(S["scn%d" % n], 1)
-        v.wait_ge(S["scn%d" % n], 1)
+            v.tensor_scalar(bt[:, r0:r1, 16 * h:16 * h + 16], T[p][:, 0:n], 0.0, None, gt).then_inc(S[sb], 1)
+        v.wait_ge(S[sb], 2)
+        v.transpose(tr[:, BLK * r0:BLK * r1], bt[:, r0:r1, :]).then_inc(S[st], 1)
 
+    v.memset(T.h4[:, :], 0.0).then_inc(S.k_z, 1)
+    v.memset(T.hb[:, 4 * HPC:], 0.0).then_inc(S.k_h, 1)
+    v.wait_ge(S.k_z, 1)
+    v.quantize_mx(T.HC[:, 0:LAND], T.HS[:, 0:LAND], T.h4[:, 0:4 * LAND]).then_inc(S.q_z, 1)
     v.memset(T.mul[:, :], 0.5).then_inc(S.k_a, 1)
     v.wait_ge(S.k_a, 1)
     for k in range(3):
         v.memset(T.mul[:, SLOT * k:FREE:BLK], 0.0).then_inc(S.k_mul, 1)
-    v.memset(T.bf[:, :, :], 0.0).then_inc(S.k_bf, 1)
-    v.wait_ge(S.l_hp, 32)
-    v.quantize_mx(T.HC[:, 0:LAND], T.HS[:, 0:LAND], T.hb[:, :]).then_inc(S.q_hp, 1)
+    v.memset(T.bf[0:BLK, :, :], 0.0).then_inc(S.k_bf, 1)
+    v.wait_ge(S.l_hp, 16)
+    v.wait_ge(S.k_h, 1)
+    v.quantize_mx(T.HQ[:, :], T.HQS[:, :], T.hb[:, :]).then_inc(S.q_hp, 1)
     for h in range(2):
         c = slice(HALF * h, HALF * h + HALF)
         v.wait_ge(S["l_e%d" % h], 16)
         v.quantize_mx(T.EC0[:, c], T.ES0[:, c], T.eb[:, 4 * HALF * h:4 * HALF * (h + 1)]).then_inc(S["q_e%d" % h], 1)
+        if h == 0:
+            v.wait_ge(S.h4c, 4)
+            v.quantize_mx(T.HC[:, OWN:], T.HS[:, OWN:], T.h4[:, 4 * LAND:]).then_inc(S.q_h4, 1)
     v.wait_ge(S.l_x, 16)
     v.quantize_mx(T.XC[:, :], T.XS[:, :], T.xb[:, :]).then_inc(S.q_x, 1)
     v.wait_ge(S.l_w, 16)
     v.quantize_mx(T.WC[:, :], T.WS[:, :], T.wb[:, :]).then_inc(S.q_w, 1)
     v.wait_ge(S.k_mul, 3)
-    buckets(0, "p0", "t_o")
-    v.tensor_scalar(T.offo[:, 0:RUNS], T.sc0[:, NBIT - 1:FREE:BLK], 256.0, None, mu).then_inc(S.off0, 1)
-    buckets(1, "p1", "t_r")
+    turn("p0", SUB, "t_o", T.bits0, 0, "bit0", T.tr0, "trn0")
+    v.wait_ge(S.trn0, 1)
+    v.tensor_tensor_scan(T.sc0[:, :], T.mul[:, 0:2 * SUB], T.tr0[:, :], 0.0, mu, ad).then_inc(S.scn0, 1)
+    v.wait_ge(S.scn0, 1)
+    q8 = SUB // 16
+    for s in range(3):
+        v.tensor_scalar(T.offo[:, q8 * s:q8 * (s + 1)], T.sc0[:, SLOT * s + NBIT - 1:2 * SUB:BLK], 256.0, None,
+                        mu).then_inc(S.off0, 1)
+    for h in range(2):
+        turn(("p1", "p4")[h], PART, "t_r%d" % h, T.bits1, RUNS // 2 * h, "bit%d" % (1 + h), T.tr1, "trn1")
+    v.wait_ge(S.trn1, 2)
+    v.tensor_tensor_scan(T.sc1[:, :], T.mul[:, :], T.tr1[:, :], 0.0, mu, ad).then_inc(S.scn1, 1)
+    v.wait_ge(S.scn1, 1)
     for k in range(3):
         v.tensor_scalar(T.offr[:, RUNS * k:RUNS * (k + 1)], T.sc1[:, SLOT * k + NBIT - 1:FREE:BLK], 256.0, None,
-                        mu).then_inc(S.off1, 1)
+                        mu).then_inc(S["off%d" % (k + 1)], 1)
     vpick(1, 0)
     v.wait_ge(S.k_bf, 1)
-    v.wait_ge(S.off0, 1)
+    for k in (0, 2, 3):
+        list_made(v, k)
     v.tensor_copy(T.bf[0:BLK, 0, 0:RUNS], T.offo[0:BLK, :]).then_inc(S.bfc, 1)
-    for k in range(1, 4):
-        v.tensor_copy(T.bf[0:BLK, k, 0:RUNS], T.offr[0:BLK, RUNS * (k - 1):RUNS * k]).then_inc(S.bfc, 1)
-    v.wait_ge(S.bfc, 4)
+    v.tensor_copy(T.bf[0:BLK, 1:4, 0:RUNS], T.offr[0:BLK, :]).then_inc(S.bfc, 1)
+    v.wait_ge(S.bfc, 2)
     v.transpose(T.tb[0:BLK, :, :], T.bf[0:BLK, :, :]).then_inc(S.v_tb, 1)
     vpick(2, 0)
     vcopy(3, 0)
     vpick(3, 0)
-
-    cp = ActivationFunctionType.Copy
 
     def acopy(k, o):
         a.wait_ge(S["t%d%d" % (k, o)], 1)
         a.activation(T["G%d%d" % (k, o)][:, 0:KCOL], T[bank[k, o]][:, 0:KCOL], cp).then_inc(S["c%d%d" % (k, o)], 1)
 
     def apick(k, o):
-        lists_made(a, k)
+        list_made(a, k)
         a.wait_ge(S["c%d%d" % (k, o)], 1)
         a.activation(T.yst[:, col(k, o)], pick(k, o), cp).then_inc(S["y%d%d" % (k, o)], 1)
 
+    a.wait_ge(S.l_hp, 16)
+    a.wait_ge(S.k_z, 1)
+    for b in range(4):
+        f = 4 * (LAND + BLK * b)
+        a.activation(T.h4[:, f:f + 4 * HPC], T.hb[:, 0:4 * HPC], cp).then_inc(S.h4c, 1)
     acopy(0, 0)
     acopy(0, 1)
     apick(0, 0)
     apick(0, 1)
     acopy(1, 0)
     acopy(1, 1)
-    apick(1, 1)
     acopy(2, 0)
     acopy(2, 1)
+    apick(1, 1)
     apick(2, 1)
     acopy(3, 1)
     apick(3, 1)

from concourse.bass import DstId, RemoteDMATransfer
from concourse.mybir import dt, AluOpType, ActivationFunctionType

TOK, NBIT, KCOL, OUT = 384, 9, 512, 2
SLOT = 10
BLK = 32
HPC = 16
LAND = 128
ZFROM = LAND + 3 * SLOT
OWN = LAND + 128
HCOLS = OWN + 128
HALF = KCOL // 2
RUNS = TOK // 16
FREE = RUNS * BLK
SUB = TOK // 3
PART = TOK // 2

_X4 = "float8_e4m3fn_x4"
SCRATCH = {
    "hb": ("sbuf", [128, 512], "bfloat16"), "h4": ("sbuf", [128, 4 * LAND + 512], "bfloat16"),
    "HQ": ("sbuf", [128, 128], _X4), "HQS": ("sbuf", [128, 128], "uint8"),
    "xb": ("sbuf", [128, 4 * TOK], "bfloat16"),
    "wb": ("sbuf", [128, 4 * 128 * OUT], "bfloat16"),
    "eb": ("sbuf", [128, 4 * KCOL], "bfloat16"),
    "HC": ("sbuf", [128, HCOLS], _X4), "HS": ("sbuf", [128, HCOLS], "uint8"),
    "XC": ("sbuf", [128, TOK], _X4), "XS": ("sbuf", [128, TOK], "uint8"),
    "WC": ("sbuf", [128, 128 * OUT], _X4), "WS": ("sbuf", [128, 128 * OUT], "uint8"),
    "mul": ("sbuf", [128, FREE], "bfloat16"),
    "bits0": ("sbuf", [128, SUB // 16, BLK], "bfloat16"), "tr0": ("sbuf", [128, 2 * SUB], "bfloat16"),
    "sc0": ("sbuf", [128, 2 * SUB], "float32"),
    "bits1": ("sbuf", [128, RUNS, BLK], "bfloat16"), "tr1": ("sbuf", [128, FREE], "bfloat16"),
    "sc1": ("sbuf", [128, FREE], "float32"),
    "bf": ("sbuf", [128, 4, BLK], "float32"), "tb": ("sbuf", [128, 4, BLK], "float32"),
    "offo": ("sbuf", [128, RUNS], "uint16"), "offr": ("sbuf", [128, 3 * RUNS], "uint16"),
    "yst": ("sbuf", [128, 4 * OUT * TOK], "float32"),
}
for _k in range(4):
    SCRATCH["EC%d" % _k] = ("sbuf", [128, KCOL], _X4)
    SCRATCH["ES%d" % _k] = ("sbuf", [128, KCOL], "uint8")
    for _o in range(OUT):
        SCRATCH["G%d%d" % (_k, _o)] = ("sbuf", [128, KCOL], "float32")
for _k in range(8):
    SCRATCH["p%d" % _k] = ("psum", [128, 512], "float32")

SEMAPHORES = (["l_hp", "l_e0", "l_e1", "l_x", "l_w", "zc", "st", "st2", "sent", "hpin", "nbin", "m0", "m1", "d0", "d1",
               "q_z", "q_hp", "q_h4", "q_e0", "q_e1", "q_x", "q_w", "k_z", "k_h", "h4c", "k_a", "k_mul", "k_bf",
               "t_o", "t_r0", "t_r1", "bfc", "v_tb",
               "bit0", "bit1", "bit2", "trn0", "trn1", "scn0", "scn1", "off0", "off1", "off2", "off3"]
              + ["t%d%d" % (k, o) for k in range(4) for o in range(OUT)]
              + ["c%d%d" % (k, o) for k in range(4) for o in range(OUT)]
              + ["y%d%d" % (k, o) for k in range(4) for o in range(OUT)])


def _bits(engines):
    return sum(1 << e for e in engines)


def rank_program(g, core, T, topo):
    rank = T.rank_of(core)
    if rank is None:
        return
    S = T.sem
    cp = ActivationFunctionType.Copy
    nb = mate = diag = None
    for c in T.cores:
        if c == core:
            continue
        if topo.chip(c) == topo.chip(core):
            nb = c
        elif topo.die(c) == topo.die(core):
            mate = c
        else:
            diag = c
    off = topo.engines(core, mate)
    on = [e for e in topo.engines(core, nb) if e not in off]
    oh = len(off) // 2
    ranks = [rank, T.rank_of(nb), T.rank_of(mate), T.rank_of(diag)]
    u8 = dt.uint8
    sent = [0]

    def cd(name, a, b):
        return T[name][:, a:b].bitcast(u8)

    def pl(name, a, b):
        return T[name][:, a:b]

    def send(*moves):
        tr = []
        for dst, eng, sem, src, out in moves:
            a = topo.addr(dst)
            tr.append(RemoteDMATransfer(dst_ids=[DstId(rid=a[0], pnc=a[1])], dma_engine_mask=_bits(eng),
                                        remote_sem=S[sem], srcs=[src], dsts=[out]))
            sent[0] += len(eng)
        g.remote_dma_fused(tr, local_sem=S.sent)

    y = g.sync
    y.dma_start(T.eb[:, 0:4 * HALF], T.e[:, 0:4 * HALF]).then_inc(S.l_e0, 16)
    y.dma_start(T.eb[:, 4 * HALF:], T.e[:, 4 * HALF:]).then_inc(S.l_e1, 16)
    y.dma_start(T.wb[:, :], T.qw[:, :]).then_inc(S.l_w, 16)
    a = g.scalar
    a.dma_start(T.hb[:, 0:4 * HPC], T.hp[:, 0:4 * HPC]).then_inc(S.l_hp, 16)
    a.dma_start(T.xb[:, :], T.x[:, :]).then_inc(S.l_x, 16)
    nz = OWN - ZFROM
    y.wait_ge(S.q_z, 1)
    y.dma_start(cd("HC", ZFROM, OWN), cd("HC", 0, nz)).then_inc(S.zc, 16)
    y.dma_start(pl("HS", ZFROM, OWN), pl("HS", 0, nz)).then_inc(S.zc, 16)

    slots = [(nb, on, 0), (mate, off[:oh], 1), (diag, off[oh:], 2)]
    g.wait_ge(S.q_hp, 1)
    for view, src, name in ((cd, "HQ", "HC"), (pl, "HQS", "HS")):
        send(*[(d, en, "hpin", view(src, 0, SLOT), view(name, LAND + SLOT * k, LAND + SLOT * (k + 1)))
               for d, en, k in slots])
    g.wait_ge(S.q_e0, 1)
    send((mate, off, "m0", cd("EC0", 0, HALF), cd("EC2", 0, HALF)), (nb, on, "nbin", cd("EC0", 0, HALF), cd("EC1", 0, HALF)))
    g.wait_ge(S.q_e1, 1)
    send((mate, off, "m1", cd("EC0", HALF, KCOL), cd("EC2", HALF, KCOL)),
         (nb, on, "nbin", cd("EC0", HALF, KCOL), cd("EC1", HALF, KCOL)))
    send((mate, off, "m1", pl("ES0", 0, KCOL), pl("ES2", 0, KCOL)), (nb, on, "nbin", pl("ES0", 0, KCOL), pl("ES1", 0, KCOL)))
    send((diag, off, "d1", cd("EC0", HALF, KCOL), cd("EC3", HALF, KCOL)))
    send((diag, off, "d1", pl("ES0", 0, KCOL), pl("ES3", 0, KCOL)))
    g.wait_ge(S.m0, len(off))
    send((nb, on, "d0", cd("EC2", 0, HALF), cd("EC3", 0, HALF)))
    g.wait_ge(S.sent, sent[0])

    t = g.tensor

    def planes(bank, moves, sem):
        for i, (f, x0, n) in enumerate(moves):
            m = t.matmul_mx(T[bank][:, 0:n], T.HC[:, f:f + 128], T.HS[:, f:f + 128], T.XC[:, x0:x0 + n], T.XS[:, x0:x0 + n],
                            i == 0, i == len(moves) - 1)
        m.then_inc(S[sem], 1)

    def tables(k, banks):
        for o in range(OUT):
            w = slice(128 * o, 128 * o + 128)
            t.matmul_mx(T[banks[o]][:, 0:KCOL], T.WC[:, w], T.WS[:, w], T["EC%d" % k][:, 0:KCOL], T["ES%d" % k][:, 0:KCOL],
                        True, True).then_inc(S["t%d%d" % (k, o)], 1)

    t.wait_ge(S.q_h4, 1)
    t.wait_ge(S.q_x, 1)
    t.wait_ge(S.q_z, 1)
    t.wait_ge(S.zc, 32)
    planes("p0", [(OWN - SLOT * s, SUB * s, SUB) for s in range(3)], "t_o")
    t.wait_ge(S.q_e0, 1)
    t.wait_ge(S.q_e1, 1)
    t.wait_ge(S.q_w, 1)
    tables(0, ("p2", "p3"))
    t.wait_ge(S.hpin, 2 * (len(on) + 2 * oh))
    for h in range(2):
        planes(("p1", "p4")[h], [(LAND - BLK * b, PART * h, PART) for b in range(4)], "t_r%d" % h)
    t.wait_ge(S.nbin, 3 * len(on))
    tables(1, ("p5", "p6"))
    t.wait_ge(S.m0, len(off))
    t.wait_ge(S.m1, 2 * len(off))
    t.wait_ge(S.bit0, 2)
    tables(2, ("p7", "p0"))
    t.wait_ge(S.c00, 1)
    t.wait_ge(S.c01, 1)
    t.wait_ge(S.d1, 2 * len(off))
    t.wait_ge(S.d0, len(on))
    tables(3, ("p2", "p3"))
    bank = {(0, 0): "p2", (0, 1): "p3", (1, 0): "p5", (1, 1): "p6", (2, 0): "p7", (2, 1): "p0", (3, 0): "p2", (3, 1): "p3"}

    def col(k, o):
        c = (ranks[k] * OUT + o) * TOK
        return slice(c, c + TOK)

    def lst(k):
        return T.offo[:, 0:RUNS] if k == 0 else T.offr[:, RUNS * (k - 1):RUNS * k]

    def pick(k, o):
        return T["G%d%d" % (k, o)][:, 0:KCOL].indirect(lst(k))

    def list_made(q, k):
        q.wait_ge(S["off%d" % k], 3 if k == 0 else 1)

    v = g.vector
    gt, mu, ad = AluOpType.is_gt, AluOpType.mult, AluOpType.add

    def vcopy(k, o):
        v.wait_ge(S["t%d%d" % (k, o)], 1)
        v.tensor_copy(T["G%d%d" % (k, o)][:, 0:KCOL], T[bank[k, o]][:, 0:KCOL]).then_inc(S["c%d%d" % (k, o)], 1)

    def vpick(k, o):
        list_made(v, k)
        v.wait_ge(S["c%d%d" % (k, o)], 1)
        v.tensor_copy(T.yst[:, col(k, o)], pick(k, o)).then_inc(S["y%d%d" % (k, o)], 1)

    def turn(p, n, sem, bt, r0, sb, tr, st):
        r1 = r0 + n // 16
        v.wait_ge(S[sem], 1)
        for h in range(2):
            v.tensor_scalar(bt[:, r0:r1, 16 * h:16 * h + 16], T[p][:, 0:n], 0.0, None, gt).then_inc(S[sb], 1)
        v.wait_ge(S[sb], 2)
        v.transpose(tr[:, BLK * r0:BLK * r1], bt[:, r0:r1, :]).then_inc(S[st], 1)

    v.memset(T.h4[:, :], 0.0).then_inc(S.k_z, 1)
    v.memset(T.hb[:, 4 * HPC:], 0.0).then_inc(S.k_h, 1)
    v.wait_ge(S.k_z, 1)
    v.quantize_mx(T.HC[:, 0:LAND], T.HS[:, 0:LAND], T.h4[:, 0:4 * LAND]).then_inc(S.q_z, 1)
    v.memset(T.mul[:, :], 0.5).then_inc(S.k_a, 1)
    v.wait_ge(S.k_a, 1)
    for k in range(3):
        v.memset(T.mul[:, SLOT * k:FREE:BLK], 0.0).then_inc(S.k_mul, 1)
    v.memset(T.bf[0:BLK, :, :], 0.0).then_inc(S.k_bf, 1)
    v.wait_ge(S.l_hp, 16)
    v.wait_ge(S.k_h, 1)
    v.quantize_mx(T.HQ[:, :], T.HQS[:, :], T.hb[:, :]).then_inc(S.q_hp, 1)
    for h in range(2):
        c = slice(HALF * h, HALF * h + HALF)
        v.wait_ge(S["l_e%d" % h], 16)
        v.quantize_mx(T.EC0[:, c], T.ES0[:, c], T.eb[:, 4 * HALF * h:4 * HALF * (h + 1)]).then_inc(S["q_e%d" % h], 1)
        if h == 0:
            v.wait_ge(S.h4c, 4)
            v.quantize_mx(T.HC[:, OWN:], T.HS[:, OWN:], T.h4[:, 4 * LAND:]).then_inc(S.q_h4, 1)
    v.wait_ge(S.l_x, 16)
    v.quantize_mx(T.XC[:, :], T.XS[:, :], T.xb[:, :]).then_inc(S.q_x, 1)
    v.wait_ge(S.l_w, 16)
    v.quantize_mx(T.WC[:, :], T.WS[:, :], T.wb[:, :]).then_inc(S.q_w, 1)
    v.wait_ge(S.k_mul, 3)
    turn("p0", SUB, "t_o", T.bits0, 0, "bit0", T.tr0, "trn0")
    v.wait_ge(S.trn0, 1)
    v.tensor_tensor_scan(T.sc0[:, :], T.mul[:, 0:2 * SUB], T.tr0[:, :], 0.0, mu, ad).then_inc(S.scn0, 1)
    v.wait_ge(S.scn0, 1)
    q8 = SUB // 16
    for s in range(3):
        v.tensor_scalar(T.offo[:, q8 * s:q8 * (s + 1)], T.sc0[:, SLOT * s + NBIT - 1:2 * SUB:BLK], 256.0, None,
                        mu).then_inc(S.off0, 1)
    for h in range(2):
        turn(("p1", "p4")[h], PART, "t_r%d" % h, T.bits1, RUNS // 2 * h, "bit%d" % (1 + h), T.tr1, "trn1")
    v.wait_ge(S.trn1, 2)
    v.tensor_tensor_scan(T.sc1[:, :], T.mul[:, :], T.tr1[:, :], 0.0, mu, ad).then_inc(S.scn1, 1)
    v.wait_ge(S.scn1, 1)
    for k in range(3):
        v.tensor_scalar(T.offr[:, RUNS * k:RUNS * (k + 1)], T.sc1[:, SLOT * k + NBIT - 1:FREE:BLK], 256.0, None,
                        mu).then_inc(S["off%d" % (k + 1)], 1)
    vpick(1, 0)
    v.wait_ge(S.k_bf, 1)
    for k in (0, 2, 3):
        list_made(v, k)
    v.tensor_copy(T.bf[0:BLK, 0, 0:RUNS], T.offo[0:BLK, :]).then_inc(S.bfc, 1)
    v.tensor_copy(T.bf[0:BLK, 1:4, 0:RUNS], T.offr[0:BLK, :]).then_inc(S.bfc, 1)
    v.wait_ge(S.bfc, 2)
    v.transpose(T.tb[0:BLK, :, :], T.bf[0:BLK, :, :]).then_inc(S.v_tb, 1)
    vpick(2, 0)
    vcopy(3, 0)
    vpick(3, 0)

    def acopy(k, o):
        a.wait_ge(S["t%d%d" % (k, o)], 1)
        a.activation(T["G%d%d" % (k, o)][:, 0:KCOL], T[bank[k, o]][:, 0:KCOL], cp).then_inc(S["c%d%d" % (k, o)], 1)

    def apick(k, o):
        list_made(a, k)
        a.wait_ge(S["c%d%d" % (k, o)], 1)
        a.activation(T.yst[:, col(k, o)], pick(k, o), cp).then_inc(S["y%d%d" % (k, o)], 1)

    a.wait_ge(S.l_hp, 16)
    a.wait_ge(S.k_z, 1)
    for b in range(4):
        f = 4 * (LAND + BLK * b)
        a.activation(T.h4[:, f:f + 4 * HPC], T.hb[:, 0:4 * HPC], cp).then_inc(S.h4c, 1)
    acopy(0, 0)
    acopy(0, 1)
    apick(0, 0)
    apick(0, 1)
    acopy(1, 0)
    acopy(1, 1)
    acopy(2, 0)
    acopy(2, 1)
    apick(1, 1)
    apick(2, 1)
    acopy(3, 1)
    apick(3, 1)
    a.wait_ge(S.y31, 1)
    a.dma_start(T.y[:, col(3, 1)], T.yst[:, col(3, 1)]).then_inc(S.st2, 16)
    a.wait_ge(S.st2, 16)

    n = [0]

    def store(k, o):
        y.wait_ge(S["y%d%d" % (k, o)], 1)
        y.dma_start(T.y[:, col(k, o)], T.yst[:, col(k, o)]).then_inc(S.st, 16)
        n[0] += 16

    for k, o in ((0, 0), (0, 1), (1, 0), (1, 1)):
        store(k, o)
    y.wait_ge(S.v_tb, 1)
    for k in range(4):
        y.dma_start(T.bk[ranks[k]:ranks[k] + 1, :], T.tb[0:RUNS, k, 0:16]).then_inc(S.st, 16)
        n[0] += 16
    for k, o in ((2, 0), (2, 1), (3, 0)):
        store(k, o)
    y.wait_ge(S.st, n[0])
